import numpy as np
import ml_dtypes


def mxq(x, axis, fmt="e4m3"):
    dtype, down = {"e4m3": (ml_dtypes.float8_e4m3fn, 7), "e5m2": (ml_dtypes.float8_e5m2, 14)}[fmt]
    v = np.moveaxis(np.asarray(x, np.float32).astype(ml_dtypes.bfloat16).astype(np.float64), axis, -1)
    blocks = v.reshape(v.shape[:-1] + (-1, 32))
    amax = np.abs(blocks).max(-1, keepdims=True)
    byte = np.maximum(np.where(amax > 0, np.frexp(amax)[1] - 1 + 127, 0) - down, 1)
    scale = np.exp2(byte - 127.0)
    codes = (blocks / scale).astype(np.float32).astype(dtype).astype(np.float64)
    return np.moveaxis((codes * scale).reshape(v.shape), -1, axis)


WIDE = False


def mx_kscale(k):
    if not WIDE:
        return np.ones(k)
    levels = np.array([10, -10, 5, -5, 0])
    if k % 512:
        return np.exp2(np.random.permutation(np.resize(levels, k // 32))).repeat(32)
    a = np.empty((k // 512, 16))
    for p in range(k // 512):
        a[p, :8] = np.random.permutation(np.resize(levels, 8))
        for g in range(8):
            far = levels[np.abs(levels - a[p, g]) >= 10]
            a[p, g + 8] = far[np.random.randint(len(far))]
    return np.exp2(a.ravel()).repeat(32)


def f64(x):
    return np.asarray(x).astype(np.float64)


def striped(idx):
    return np.tile(idx.reshape(-1, 16).T, (8, 1)).astype(np.uint16)


def unstriped(offs):
    return offs[:16].T.reshape(-1).astype(np.int64)


def pack_weight(w):
    k, n = w.shape
    w = f64(np.asarray(w, np.float32).astype(ml_dtypes.bfloat16)).reshape(k // 32, 32, n)
    amax = np.abs(w).max(1)
    byte = np.clip(np.where(amax > 0, np.frexp(amax)[1] - 1 + 127 - 7, 1), 1, 254)
    scaled = (w * np.exp2(127.0 - byte)[:, None, :]).reshape(k, n).astype(np.float32)
    words = np.ascontiguousarray(scaled.reshape(k // 512, 128, 4, n).transpose(0, 1, 3, 2)).astype(ml_dtypes.float8_e4m3fn).view(np.uint8)
    return words, np.ascontiguousarray(byte.astype(np.uint8).reshape(k // 512, 16, n))


def unpack_weight(words, scales):
    g, p, n, _ = words.shape
    vals = np.ascontiguousarray(words).view(ml_dtypes.float8_e4m3fn).astype(np.float64) * np.repeat(np.exp2(scales.astype(np.float64) - 127.0), 8, axis=1)[..., None]
    return vals.transpose(0, 1, 3, 2).reshape(g * 512, n)


K, T, E, C, N = 1536, 1024, 16, 128, 128


def by_expert(wq, xq):
    return np.concatenate([wq[e].T @ xq[:, e * C:(e + 1) * C] for e in range(E)], axis=1)


def setup_inputs():
    n = np.random.standard_normal
    s = mx_kscale(K)[:, None]
    first = np.random.permutation(np.repeat(np.arange(E), T // E))
    second = (first + 1 + np.random.permutation(np.repeat(np.arange(E - 1), -(-T // (E - 1)))[:T])) % E
    while np.bincount(second, minlength=E).max() != T // E:
        load = np.bincount(second, minlength=E); hi, lo = int(load.argmax()), int(load.argmin())
        t = np.flatnonzero((second == hi) & (first != lo))[0]; second[t] = lo
    slot_token = np.empty(E * C, np.int64); pos = np.empty((2, T), np.int64); fill = np.zeros(E, np.int64)
    place = np.stack([np.random.permutation(C) for _ in range(E)])
    for r, deal in enumerate((first, second)):
        for t in np.random.permutation(T):
            e = deal[t]; j = e * C + place[e, fill[e]]; fill[e] += 1; slot_token[j] = t; pos[r, t] = j
    g = np.random.uniform(0.2, 0.8, T)
    packed = [pack_weight(m) for m in n((E, K, N)) / np.sqrt(K) / s[None]]
    return {
        "xT": (n((K, T)) * s).astype(np.float32),
        "w_words": np.stack([m[0] for m in packed]),
        "w_scales": np.stack([m[1] for m in packed]),
        "gate": np.stack([np.tile(g, (N, 1)), np.tile(1.0 - g, (N, 1))]).astype(np.float32),
        "offs": striped(slot_token),
        "pos1": striped(pos[0]),
        "pos2": striped(pos[1]),
    }


def reference(xT, w_words, w_scales, gate, offs, pos1, pos2):
    idx = unstriped(offs)
    xq = mxq(f64(xT)[:, idx], 0, "e4m3")
    w = np.stack([unpack_weight(w_words[e], w_scales[e]) for e in range(E)])
    y = by_expert(w, xq)
    return f64(gate[0]) * y[:, unstriped(pos1)] + f64(gate[1]) * y[:, unstriped(pos2)]

@@ -1,0 +1,140 @@
+from contextlib import ExitStack
+
+import concourse.mybir as mybir
+
+K, T, E, C, N = 1536, 1024, 16, 128, 128
+FLOPS = 2 * K * N * E * C
+
+F32 = mybir.dt.float32
+BF16 = mybir.dt.bfloat16
+I32 = mybir.dt.int32
+U32 = mybir.dt.uint32
+U16 = mybir.dt.uint16
+U8 = mybir.dt.uint8
+FP8X4 = mybir.dt.float8_e4m3fn_x4
+MULT = mybir.AluOpType.mult
+ADD = mybir.AluOpType.add
+
+P = 128
+PASSES = K // 512
+LOADS = ((256, 256, 256, 256), (512, 512), (512, 512))
+QUANT = (256, 512, 512)
+VCOLS = (160, 0, 0)
+CHUNKS = (6, 6, 4)
+
+
+def tile_routed_moe_kernel(tc, xT, w_words, w_scales, gate, offs, pos1, pos2, out):
+    nc = tc.nc
+    with ExitStack() as ctx:
+        keep = ctx.enter_context(tc.tile_pool(name="keep", bufs=1))
+        psum = ctx.enter_context(tc.psum_pool(name="psum", bufs=1))
+
+        offs_sb = keep.tile([P, E * C // 16], U16, name="offs_sb")
+        pos_sb = [keep.tile([P, T // 16], U16, name=f"pos{i}_sb") for i in (1, 2)]
+        x_pass = xT.rearrange("(g p t) n -> g p t n", p=P, t=4)
+
+        raw = []
+        for a in range(PASSES):
+            parts = []
+            col = 0
+            for i, width in enumerate(LOADS[a]):
+                r = keep.tile([P, 4, width], F32, name=f"raw{a}_{i}")
+                nc.sync.dma_start(r[:], x_pass[a, :, :, col : col + width])
+                if a == 0 and i == 0:
+                    nc.sync.dma_start(offs_sb[:], offs)
+                parts.append((col, width, r))
+                col += width
+            raw.append(parts)
+
+        w_scale = keep.tile([P, E * PASSES, N], U8, name="w_scale", align_bytes=64)
+        nc.vector.memset(w_scale[:].rearrange("p e n -> p (e n)").bitcast(I32), 0)
+        for q in range(4):
+            nc.sync.dma_start(
+                w_scale[32 * q : 32 * q + 4].bitcast(I32),
+                w_scales[:, :, 4 * q : 4 * q + 4, :].rearrange("e a q n -> q (e a) n").bitcast(I32),
+            )
+        w_code = []
+        e0 = 0
+        for c, ne in enumerate(CHUNKS):
+            w = keep.tile([P, ne * PASSES, N], U32, name=f"w_code{c}", align_bytes=64)
+            nc.sync.dma_start(w[:].bitcast(I32), w_words[e0 : e0 + ne].rearrange("e a p n r -> p (e a) (n r)").bitcast(I32))
+            w_code.append(w)
+            e0 += ne
+        gate_sb = [keep.tile([P, T], F32, name=f"gate{i}_sb") for i in (1, 2)]
+        for i in range(2):
+            nc.sync.dma_start(gate_sb[i][:], gate[i])
+        nc.sync.dma_start(pos_sb[0][:], pos1)
+        nc.sync.dma_start(pos_sb[1][:], pos2)
+
+        x_scale = keep.tile([P, T], U8, name="x_scale", align_bytes=64)
+        nc.gpsimd.memset(x_scale[:], 0)
+        x_code = [keep.tile([P, T], U32, name=f"x_code{a}", align_bytes=64) for a in range(PASSES)]
+        slot_code = [
+            [keep.tile([P, ne * C], U32, name=f"slot_code{a}_{c}", align_bytes=64) for c, ne in enumerate(CHUNKS)]
+            for a in range(PASSES)
+        ]
+        slot_scale = [keep.tile([P, ne * C], U8, name=f"slot_scale{c}", align_bytes=64) for c, ne in enumerate(CHUNKS)]
+        first = [sum(CHUNKS[:c]) for c in range(len(CHUNKS))]
+        lists = [offs_sb[:, first[c] * C // 16 : (first[c] + ne) * C // 16] for c, ne in enumerate(CHUNKS)]
+
+        for a in range(PASSES):
+            width_q = QUANT[a]
+            for b in range(T // width_q):
+                xb = keep.tile([P, width_q, 4], BF16, name=f"xb{a}_{b}", align_bytes=64)
+                for col, width, r in raw[a]:
+                    lo, hi = max(col, b * width_q), min(col + width, (b + 1) * width_q)
+                    if lo >= hi:
+                        continue
+                    mid = lo + VCOLS[a]
+                    for engine, c0, c1 in ((nc.vector.tensor_copy, lo, mid), (nc.scalar.copy, mid, hi)):
+                        if c0 < c1:
+                            engine(
+                                xb[:, c0 - b * width_q : c1 - b * width_q, :],
+                                r[:, :, c0 - col : c1 - col].rearrange("p t n -> p n t"),
+                            )
+                cols = slice(b * width_q, (b + 1) * width_q)
+                nc.vector.quantize_mx(
+                    out=x_code[a][:, cols].bitcast(FP8X4),
+                    scales=x_scale[4 * a : P, cols],
+                    in_=xb[:].rearrange("p n t -> p (n t)"),
+                )
+            if a < PASSES - 1:
+                for c in range(len(CHUNKS)):
+                    nc.vector.tensor_copy(slot_code[a][c][:], x_code[a][:].indirect(lists[c]))
+
+        y = keep.tile([P, E * C], F32, name="y")
+        for c, ne in enumerate(CHUNKS):
+            nc.vector.tensor_copy(slot_scale[c][:], x_scale[:].indirect(lists[c]))
+            nc.vector.tensor_copy(slot_code[PASSES - 1][c][:], x_code[PASSES - 1][:].indirect(lists[c]))
+            for j0 in range(0, ne, 4):
+                n = min(4, ne - j0)
+                acc = psum.tile([P, n * C], F32, name=f"acc{c}_{j0}")
+                for j in range(n):
+                    e = j0 + j
+                    cols = slice(e * C, (e + 1) * C)
+                    for a in range(PASSES):
+                        nc.tensor.matmul_mx(
+                            out=acc[:, j * C : (j + 1) * C],
+                            lhsT=w_code[c][:, e * PASSES + a, :].bitcast(FP8X4),
+                            lhsT_scale=w_scale[:, (first[c] + e) * PASSES + a, :],
+                            rhs=slot_code[a][c][:, cols].bitcast(FP8X4),
+                            rhs_scale=slot_scale[c][4 * a : P, cols],
+                            start=(a == 0),
+                            stop=(a == PASSES - 1),
+                        )
+                base = (first[c] + j0) * C
+                nc.scalar.copy(y[:, base : base + n * C], acc[:])
+
+        half = T // 2
+        for h in range(2):
+            cols = slice(h * half, (h + 1) * half)
+            part = []
+            for i in range(2):
+                g = keep.tile([P, half], F32, name=f"part{i}_{h}")
+                nc.vector.tensor_tensor(
+                    g[:], y[:].indirect(pos_sb[i][:, h * half // 16 : (h + 1) * half // 16]), gate_sb[i][:, cols], MULT
+                )
+                part.append(g)
+            total = keep.tile([P, half], F32, name=f"total{h}")
+            nc.vector.tensor_tensor(total[:], part[0][:], part[1][:], ADD)
+            nc.sync.dma_start(out[:, cols], total[:])

@@ -17,10 +17,17 @@ ADD = mybir.AluOpType.add
 
 P = 128
 PASSES = K // 512
-LOADS = ((256, 256, 256, 256), (512, 512), (512, 512))
-QUANT = (256, 512, 512)
-VCOLS = (160, 0, 0)
-CHUNKS = (6, 6, 4)
+LOADS = ((512, 256, 256), (512, 512), (512, 512))
+CASTS = ((("V", 0, 320), ("S", 320, 512), ("V", 512, 672), ("S", 672, 768), ("V", 768, 928), ("S", 928, 1024)), (("S", 0, 512), ("S", 512, 768), ("S", 768, 1024)), (("S", 0, 512), ("S", 512, 768), ("S", 768, 1024)))
+QUANT = ((512, 256, 256), (512, 512), (512, 512))
+WORDS = ((12, 4), (12, 4), (6, 6, 3, 1))
+BYTES_CUT = (12, 4)
+SEQ = ("q0", "w00", "w01", "q1", "w10", "w11", "q2", "b0", "w20", "w21", "b1", "w22", "w23")
+GROUPS = ((4, "S"), (2, "S"), (4, "S"), (2, "S"), (3, "S"), (1, "V"))
+WLOADS = (6, 6, 4)
+PARTS = (768, 256)
+WINDOWS = (2048, 2048, 1024)
+SCALE_WINDOW = 2048
 
 
 def tile_routed_moe_kernel(tc, xT, w_words, w_scales, gate, offs, pos1, pos2, out):
@@ -32,6 +39,21 @@ def tile_routed_moe_kernel(tc, xT, w_words, w_scales, gate, offs, pos1, pos2, ou
         offs_sb = keep.tile([P, E * C // 16], U16, name="offs_sb")
         pos_sb = [keep.tile([P, T // 16], U16, name=f"pos{i}_sb") for i in (1, 2)]
         x_pass = xT.rearrange("(g p t) n -> g p t n", p=P, t=4)
+        x_code = [keep.tile([P, WINDOWS[a]], I32, name=f"x_code{a}", align_bytes=64) for a in range(PASSES)]
+        x_scale = keep.tile([P, SCALE_WINDOW], U8, name="x_scale", align_bytes=64)
+        w_scale = keep.tile([P, E, PASSES, N], U8, name="w_scale", align_bytes=64)
+        nc.gpsimd.memset(x_scale[:], 0)
+        for a in range(PASSES):
+            if WINDOWS[a] > T:
+                nc.vector.memset(x_code[a][:, T:], 0)
+        nc.gpsimd.memset(w_scale[:].rearrange("p e a n -> p (e a n)").bitcast(I32), 0)
+
+        def load_scales():
+            for q in range(4):
+                nc.sync.dma_start(
+                    w_scale[32 * q : 32 * q + 4].rearrange("p e a n -> p (e a) n").bitcast(I32),
+                    w_scales[:, :, 4 * q : 4 * q + 4, :].rearrange("e a q n -> q (e a) n").bitcast(I32),
+                )
 
         raw = []
         for a in range(PASSES):
@@ -46,95 +68,98 @@ def tile_routed_moe_kernel(tc, xT, w_words, w_scales, gate, offs, pos1, pos2, ou
                 col += width
             raw.append(parts)
 
-        w_scale = keep.tile([P, E * PASSES, N], U8, name="w_scale", align_bytes=64)
-        nc.vector.memset(w_scale[:].rearrange("p e n -> p (e n)").bitcast(I32), 0)
-        for q in range(4):
-            nc.sync.dma_start(
-                w_scale[32 * q : 32 * q + 4].bitcast(I32),
-                w_scales[:, :, 4 * q : 4 * q + 4, :].rearrange("e a q n -> q (e a) n").bitcast(I32),
-            )
-        w_code = []
+        w_at = []
         e0 = 0
-        for c, ne in enumerate(CHUNKS):
+        for c, ne in enumerate(WLOADS):
+            if c == 0:
+                load_scales()
             w = keep.tile([P, ne * PASSES, N], U32, name=f"w_code{c}", align_bytes=64)
             nc.sync.dma_start(w[:].bitcast(I32), w_words[e0 : e0 + ne].rearrange("e a p n r -> p (e a) (n r)").bitcast(I32))
-            w_code.append(w)
+            w_at += [(w, j) for j in range(ne)]
             e0 += ne
+            if c == 0:
+                nc.sync.dma_start(pos_sb[0][:], pos1)
+                nc.sync.dma_start(pos_sb[1][:], pos2)
         gate_sb = [keep.tile([P, T], F32, name=f"gate{i}_sb") for i in (1, 2)]
         for i in range(2):
             nc.sync.dma_start(gate_sb[i][:], gate[i])
-        nc.sync.dma_start(pos_sb[0][:], pos1)
-        nc.sync.dma_start(pos_sb[1][:], pos2)
 
-        x_scale = keep.tile([P, T], U8, name="x_scale", align_bytes=64)
-        nc.gpsimd.memset(x_scale[:], 0)
-        x_code = [keep.tile([P, T], U32, name=f"x_code{a}", align_bytes=64) for a in range(PASSES)]
-        slot_code = [
-            [keep.tile([P, ne * C], U32, name=f"slot_code{a}_{c}", align_bytes=64) for c, ne in enumerate(CHUNKS)]
-            for a in range(PASSES)
-        ]
-        slot_scale = [keep.tile([P, ne * C], U8, name=f"slot_scale{c}", align_bytes=64) for c, ne in enumerate(CHUNKS)]
-        first = [sum(CHUNKS[:c]) for c in range(len(CHUNKS))]
-        lists = [offs_sb[:, first[c] * C // 16 : (first[c] + ne) * C // 16] for c, ne in enumerate(CHUNKS)]
+        code_at = [[] for a in range(PASSES)]
+        scale_at = []
 
-        for a in range(PASSES):
-            width_q = QUANT[a]
-            for b in range(T // width_q):
-                xb = keep.tile([P, width_q, 4], BF16, name=f"xb{a}_{b}", align_bytes=64)
-                for col, width, r in raw[a]:
-                    lo, hi = max(col, b * width_q), min(col + width, (b + 1) * width_q)
-                    if lo >= hi:
+        def gather(window, cuts, c, dtype, name, where):
+            e0, ne = sum(cuts[:c]), cuts[c]
+            g = keep.tile([P, ne * C], dtype, name=name, align_bytes=64)
+            nc.vector.tensor_copy(g[:], window.indirect(offs_sb[:, e0 * C // 16 : (e0 + ne) * C // 16]))
+            where.extend((g, j * C) for j in range(ne))
+
+        def quantise(a):
+            q0 = 0
+            for b, width in enumerate(QUANT[a]):
+                xb = keep.tile([P, width, 4], BF16, name=f"xb{a}_{b}", align_bytes=64)
+                for engine, lo, hi in CASTS[a]:
+                    if not (q0 <= lo < q0 + width):
                         continue
-                    mid = lo + VCOLS[a]
-                    for engine, c0, c1 in ((nc.vector.tensor_copy, lo, mid), (nc.scalar.copy, mid, hi)):
-                        if c0 < c1:
-                            engine(
-                                xb[:, c0 - b * width_q : c1 - b * width_q, :],
-                                r[:, :, c0 - col : c1 - col].rearrange("p t n -> p n t"),
+                    for col, wd, r in raw[a]:
+                        if col <= lo < col + wd:
+                            copy = nc.vector.tensor_copy if engine == "V" else nc.scalar.copy
+                            copy(
+                                xb[:, lo - q0 : hi - q0, :].rearrange("p (c i) t -> p c t i", i=4),
+                                r[:, :, lo - col : hi - col].rearrange("p t (c i) -> p c t i", i=4),
                             )
-                cols = slice(b * width_q, (b + 1) * width_q)
+                cols = slice(q0, q0 + width)
                 nc.vector.quantize_mx(
                     out=x_code[a][:, cols].bitcast(FP8X4),
                     scales=x_scale[4 * a : P, cols],
                     in_=xb[:].rearrange("p n t -> p (n t)"),
                 )
-            if a < PASSES - 1:
-                for c in range(len(CHUNKS)):
-                    nc.vector.tensor_copy(slot_code[a][c][:], x_code[a][:].indirect(lists[c]))
+                q0 += width
 
         y = keep.tile([P, E * C], F32, name="y")
-        for c, ne in enumerate(CHUNKS):
-            nc.vector.tensor_copy(slot_scale[c][:], x_scale[:].indirect(lists[c]))
-            nc.vector.tensor_copy(slot_code[PASSES - 1][c][:], x_code[PASSES - 1][:].indirect(lists[c]))
-            for j0 in range(0, ne, 4):
-                n = min(4, ne - j0)
-                acc = psum.tile([P, n * C], F32, name=f"acc{c}_{j0}")
+        last = PASSES - 1
+        group = 0
+        done = 0
+        for what in SEQ:
+            if what[0] == "q":
+                quantise(int(what[1]))
+            elif what[0] == "b":
+                gather(x_scale[:], BYTES_CUT, int(what[1]), U8, f"slot_scale{what[1]}", scale_at)
+            else:
+                a = int(what[1])
+                gather(x_code[a][:].bitcast(U32), WORDS[a], int(what[2]), U32, f"slot_code{a}_{what[2]}", code_at[a])
+            ready = min(len(code_at[0]), len(code_at[1]), len(code_at[2]), len(scale_at))
+            while group < len(GROUPS) and done + GROUPS[group][0] <= ready:
+                n, engine = GROUPS[group]
+                acc = psum.tile([P, n * C], F32, name=f"acc{group}")
                 for j in range(n):
-                    e = j0 + j
-                    cols = slice(e * C, (e + 1) * C)
+                    e = done + j
+                    sc, s0 = scale_at[e]
+                    w, wj = w_at[e]
                     for a in range(PASSES):
+                        co, c0 = code_at[a][e]
                         nc.tensor.matmul_mx(
                             out=acc[:, j * C : (j + 1) * C],
-                            lhsT=w_code[c][:, e * PASSES + a, :].bitcast(FP8X4),
-                            lhsT_scale=w_scale[:, (first[c] + e) * PASSES + a, :],
-                            rhs=slot_code[a][c][:, cols].bitcast(FP8X4),
-                            rhs_scale=slot_scale[c][4 * a : P, cols],
+                            lhsT=w[:, wj * PASSES + a, :].bitcast(FP8X4),
+                            lhsT_scale=w_scale[:, e, a, :],
+                            rhs=co[:, c0 : c0 + C].bitcast(FP8X4),
+                            rhs_scale=sc[4 * a : P, s0 : s0 + C],
                             start=(a == 0),
                             stop=(a == PASSES - 1),
                         )
-                base = (first[c] + j0) * C
-                nc.scalar.copy(y[:, base : base + n * C], acc[:])
+                copy = nc.vector.tensor_copy if engine == "V" else nc.scalar.copy
+                copy(y[:, done * C : (done + n) * C], acc[:])
+                done += n
+                group += 1
 
-        half = T // 2
-        for h in range(2):
-            cols = slice(h * half, (h + 1) * half)
+        t0 = 0
+        for h, width in enumerate(PARTS):
+            cols = slice(t0, t0 + width)
             part = []
             for i in range(2):
-                g = keep.tile([P, half], F32, name=f"part{i}_{h}")
-                nc.vector.tensor_tensor(
-                    g[:], y[:].indirect(pos_sb[i][:, h * half // 16 : (h + 1) * half // 16]), gate_sb[i][:, cols], MULT
-                )
+                g = keep.tile([P, width], F32, name=f"part{i}_{h}")
+                nc.vector.tensor_tensor(g[:], y[:].indirect(pos_sb[i][:, t0 // 16 : (t0 + width) // 16]), gate_sb[i][:, cols], MULT)
                 part.append(g)
-            total = keep.tile([P, half], F32, name=f"total{h}")
+            total = keep.tile([P, width], F32, name=f"total{h}")
             nc.vector.tensor_tensor(total[:], part[0][:], part[1][:], ADD)
             nc.sync.dma_start(out[:, cols], total[:])
+            t0 += width

@@ -18,8 +18,8 @@ ADD = mybir.AluOpType.add
 P = 128
 PASSES = K // 512
 LOADS = ((512, 256, 256), (512, 512), (512, 512))
-CASTS = ((("V", 0, 320), ("S", 320, 512), ("V", 512, 672), ("S", 672, 768), ("V", 768, 928), ("S", 928, 1024)), (("S", 0, 512), ("S", 512, 768), ("S", 768, 1024)), (("S", 0, 512), ("S", 512, 768), ("S", 768, 1024)))
-QUANT = ((512, 256, 256), (512, 512), (512, 512))
+CASTS = ((("V", 0, 320), ("S", 320, 512), ("V", 512, 672), ("S", 672, 768), ("V", 768, 928), ("S", 928, 1024)), (("S", 0, 512), ("S", 512, 768), ("V", 768, 1024)), (("S", 0, 512), ("S", 512, 768), ("S", 768, 1024)))
+QUANT = ((512, 256, 256), (512, 256, 256), (512, 512))
 WORDS = ((12, 4), (12, 4), (6, 6, 3, 1))
 BYTES_CUT = (12, 4)
 SEQ = ("q0", "w00", "w01", "q1", "w10", "w11", "q2", "b0", "w20", "w21", "b1", "w22", "w23")
@@ -34,12 +34,13 @@ def tile_routed_moe_kernel(tc, xT, w_words, w_scales, gate, offs, pos1, pos2, ou
     nc = tc.nc
     with ExitStack() as ctx:
         keep = ctx.enter_context(tc.tile_pool(name="keep", bufs=1))
+        turn = ctx.enter_context(tc.tile_pool(name="turn", bufs=1))
         psum = ctx.enter_context(tc.psum_pool(name="psum", bufs=1))
 
         offs_sb = keep.tile([P, E * C // 16], U16, name="offs_sb")
         pos_sb = [keep.tile([P, T // 16], U16, name=f"pos{i}_sb") for i in (1, 2)]
         x_pass = xT.rearrange("(g p t) n -> g p t n", p=P, t=4)
-        x_code = [keep.tile([P, WINDOWS[a]], I32, name=f"x_code{a}", align_bytes=64) for a in range(PASSES)]
+        x_code = [(turn if a == 0 else keep).tile([P, WINDOWS[a]], I32, name=f"x_code{a}", tag="turn" if a == 0 else f"x_code{a}", align_bytes=64) for a in range(PASSES)]
         x_scale = keep.tile([P, SCALE_WINDOW], U8, name="x_scale", align_bytes=64)
         w_scale = keep.tile([P, E, PASSES, N], U8, name="w_scale", align_bytes=64)
         nc.gpsimd.memset(x_scale[:], 0)
@@ -96,7 +97,8 @@ def tile_routed_moe_kernel(tc, xT, w_words, w_scales, gate, offs, pos1, pos2, ou
         def quantise(a):
             q0 = 0
             for b, width in enumerate(QUANT[a]):
-                xb = keep.tile([P, width, 4], BF16, name=f"xb{a}_{b}", align_bytes=64)
+                shared = (a, b) == (1, 2)
+                xb = (turn if shared else keep).tile([P, width, 4], BF16, name=f"xb{a}_{b}", tag="turn" if shared else f"xb{a}_{b}", align_bytes=64)
                 for engine, lo, hi in CASTS[a]:
                     if not (q0 <= lo < q0 + width):
                         continue

@@ -17,15 +17,16 @@ ADD = mybir.AluOpType.add
 
 P = 128
 PASSES = K // 512
-LOADS = ((512, 256, 256), (512, 512), (512, 512))
-CASTS = ((("V", 0, 320), ("S", 320, 512), ("V", 512, 672), ("S", 672, 768), ("V", 768, 928), ("S", 928, 1024)), (("S", 0, 512), ("S", 512, 768), ("V", 768, 1024)), (("S", 0, 512), ("S", 512, 768), ("S", 768, 1024)))
-QUANT = ((512, 256, 256), (512, 256, 256), (512, 512))
+LOADS = ((512, 256, 128, 128), (256, 256, 512), (512, 512))
+CASTS = ((("V", 0, 320), ("S", 320, 512), ("V", 512, 672), ("S", 672, 768), ("V", 768, 848), ("S", 848, 896), ("V", 896, 976), ("S", 976, 1024)), (("S", 0, 256), ("S", 256, 512), ("S", 512, 768), ("S", 768, 896), ("V", 896, 1024)), (("S", 0, 512), ("S", 512, 768), ("S", 768, 1024)))
+QUANT = ((512, 256, 128, 128), (512, 256, 128, 128), (512, 256, 256))
 WORDS = ((12, 4), (12, 4), (6, 6, 3, 1))
 BYTES_CUT = (12, 4)
 SEQ = ("q0", "w00", "w01", "q1", "w10", "w11", "q2", "b0", "w20", "w21", "b1", "w22", "w23")
 GROUPS = ((4, "S"), (2, "S"), (4, "S"), (2, "S"), (3, "S"), (1, "V"))
 WLOADS = (6, 6, 4)
 PARTS = (768, 256)
+SHARED = (1, 3)
 WINDOWS = (2048, 2048, 1024)
 SCALE_WINDOW = 2048
 
@@ -63,7 +64,7 @@ def tile_routed_moe_kernel(tc, xT, w_words, w_scales, gate, offs, pos1, pos2, ou
             for i, width in enumerate(LOADS[a]):
                 r = keep.tile([P, 4, width], F32, name=f"raw{a}_{i}")
                 nc.sync.dma_start(r[:], x_pass[a, :, :, col : col + width])
-                if a == 0 and i == 0:
+                if a == 0 and i == len(LOADS[0]) - 1:
                     nc.sync.dma_start(offs_sb[:], offs)
                 parts.append((col, width, r))
                 col += width
@@ -97,7 +98,7 @@ def tile_routed_moe_kernel(tc, xT, w_words, w_scales, gate, offs, pos1, pos2, ou
         def quantise(a):
             q0 = 0
             for b, width in enumerate(QUANT[a]):
-                shared = (a, b) == (1, 2)
+                shared = (a, b) == SHARED
                 xb = (turn if shared else keep).tile([P, width, 4], BF16, name=f"xb{a}_{b}", tag="turn" if shared else f"xb{a}_{b}", align_bytes=64)
                 for engine, lo, hi in CASTS[a]:
                     if not (q0 <= lo < q0 + width):
@@ -153,15 +154,23 @@ def tile_routed_moe_kernel(tc, xT, w_words, w_scales, gate, offs, pos1, pos2, ou
                 done += n
                 group += 1
 
-        t0 = 0
-        for h, width in enumerate(PARTS):
-            cols = slice(t0, t0 + width)
-            part = []
-            for i in range(2):
-                g = keep.tile([P, width], F32, name=f"part{i}_{h}")
-                nc.vector.tensor_tensor(g[:], y[:].indirect(pos_sb[i][:, t0 // 16 : (t0 + width) // 16]), gate_sb[i][:, cols], MULT)
-                part.append(g)
-            total = keep.tile([P, width], F32, name=f"total{h}")
-            nc.vector.tensor_tensor(total[:], part[0][:], part[1][:], ADD)
-            nc.sync.dma_start(out[:, cols], total[:])
-            t0 += width
+        def fetch(i, h):
+            g = keep.tile([P, PARTS[h]], F32, name=f"part{i}_{h}")
+            t = sum(PARTS[:h])
+            nc.vector.tensor_tensor(
+                g[:], y[:].indirect(pos_sb[i][:, t // 16 : (t + PARTS[h]) // 16]), gate_sb[i][:, t : t + PARTS[h]], MULT
+            )
+            return g
+
+        def finish(h, first, second):
+            t = sum(PARTS[:h])
+            total = keep.tile([P, PARTS[h]], F32, name=f"total{h}")
+            nc.vector.tensor_tensor(total[:], first[:], second[:], ADD)
+            nc.sync.dma_start(out[:, t : t + PARTS[h]], total[:])
+
+        a1 = fetch(0, 0)
+        a2 = fetch(1, 0)
+        b1 = fetch(0, 1)
+        finish(0, a1, a2)
+        b2 = fetch(1, 1)
+        finish(1, b1, b2)

@@ -17,13 +17,13 @@ ADD = mybir.AluOpType.add
 
 P = 128
 PASSES = K // 512
-LOADS = ((512, 256, 128, 128), (256, 256, 512), (512, 512))
-CASTS = ((("V", 0, 320), ("S", 320, 512), ("V", 512, 672), ("S", 672, 768), ("V", 768, 848), ("S", 848, 896), ("V", 896, 976), ("S", 976, 1024)), (("S", 0, 256), ("S", 256, 512), ("S", 512, 768), ("S", 768, 896), ("V", 896, 1024)), (("S", 0, 512), ("S", 512, 768), ("S", 768, 1024)))
-QUANT = ((512, 256, 128, 128), (512, 256, 128, 128), (512, 256, 256))
+LOADS = ((512, 256, 256), (256, 256, 512), (512, 512))
+CASTS = ((("V", 0, 320), ("S", 320, 512), ("V", 512, 672), ("S", 672, 768), ("V", 768, 928), ("S", 928, 1024)), (("S", 0, 256), ("S", 256, 512), ("S", 512, 768), ("S", 768, 896), ("V", 896, 1024)), (("S", 0, 512), ("S", 512, 768), ("S", 768, 1024)))
+QUANT = ((512, 256, 256), (512, 256, 128, 128), (512, 256, 256))
 WORDS = ((12, 4), (12, 4), (6, 6, 3, 1))
-BYTES_CUT = (12, 4)
-SEQ = ("q0", "w00", "w01", "q1", "w10", "w11", "q2", "b0", "w20", "w21", "b1", "w22", "w23")
-GROUPS = ((4, "S"), (2, "S"), (4, "S"), (2, "S"), (3, "S"), (1, "V"))
+BYTES_CUT = (6, 6, 4)
+SEQ = ("q0", "w00", "w01", "q1", "w10", "w11", "q2", "b0", "w20", "b1", "w21", "b2", "w22", "w23")
+VECTOR_COPIES = (15,)
 WLOADS = (6, 6, 4)
 PARTS = (768, 256)
 SHARED = (1, 3)
@@ -120,39 +120,42 @@ def tile_routed_moe_kernel(tc, xT, w_words, w_scales, gate, offs, pos1, pos2, ou
 
         y = keep.tile([P, E * C], F32, name="y")
         last = PASSES - 1
-        group = 0
-        done = 0
+        accs = []
+
+        def multiply(e, passes):
+            sc, s0 = scale_at[e]
+            w, wj = w_at[e]
+            for a in passes:
+                co, c0 = code_at[a][e]
+                nc.tensor.matmul_mx(
+                    out=accs[e][:],
+                    lhsT=w[:, wj * PASSES + a, :].bitcast(FP8X4),
+                    lhsT_scale=w_scale[:, e, a, :],
+                    rhs=co[:, c0 : c0 + C].bitcast(FP8X4),
+                    rhs_scale=sc[4 * a : P, s0 : s0 + C],
+                    start=(a == 0),
+                    stop=(a == last),
+                )
+
         for what in SEQ:
             if what[0] == "q":
                 quantise(int(what[1]))
             elif what[0] == "b":
+                e0 = len(scale_at)
                 gather(x_scale[:], BYTES_CUT, int(what[1]), U8, f"slot_scale{what[1]}", scale_at)
+                for e in range(e0, len(scale_at)):
+                    acc = psum.tile([P, C], F32, name=f"acc{e}", tag=f"bank{e % 8}")
+                    accs.append(acc)
+                    multiply(e, range(last))
             else:
                 a = int(what[1])
+                e0 = len(code_at[a])
                 gather(x_code[a][:].bitcast(U32), WORDS[a], int(what[2]), U32, f"slot_code{a}_{what[2]}", code_at[a])
-            ready = min(len(code_at[0]), len(code_at[1]), len(code_at[2]), len(scale_at))
-            while group < len(GROUPS) and done + GROUPS[group][0] <= ready:
-                n, engine = GROUPS[group]
-                acc = psum.tile([P, n * C], F32, name=f"acc{group}")
-                for j in range(n):
-                    e = done + j
-                    sc, s0 = scale_at[e]
-                    w, wj = w_at[e]
-                    for a in range(PASSES):
-                        co, c0 = code_at[a][e]
-                        nc.tensor.matmul_mx(
-                            out=acc[:, j * C : (j + 1) * C],
-                            lhsT=w[:, wj * PASSES + a, :].bitcast(FP8X4),
-                            lhsT_scale=w_scale[:, e, a, :],
-                            rhs=co[:, c0 : c0 + C].bitcast(FP8X4),
-                            rhs_scale=sc[4 * a : P, s0 : s0 + C],
-                            start=(a == 0),
-                            stop=(a == PASSES - 1),
-                        )
-                copy = nc.vector.tensor_copy if engine == "V" else nc.scalar.copy
-                copy(y[:, done * C : (done + n) * C], acc[:])
-                done += n
-                group += 1
+                if a == last:
+                    for e in range(e0, len(code_at[a])):
+                        multiply(e, [last])
+                        copy = nc.vector.tensor_copy if e in VECTOR_COPIES else nc.scalar.copy
+                        copy(y[:, e * C : (e + 1) * C], accs[e][:])
 
         def fetch(i, h):
             g = keep.tile([P, PARTS[h]], F32, name=f"part{i}_{h}")
@@ -162,15 +165,17 @@ def tile_routed_moe_kernel(tc, xT, w_words, w_scales, gate, offs, pos1, pos2, ou
             )
             return g
 
-        def finish(h, first, second):
-            t = sum(PARTS[:h])
-            total = keep.tile([P, PARTS[h]], F32, name=f"total{h}")
-            nc.vector.tensor_tensor(total[:], first[:], second[:], ADD)
-            nc.sync.dma_start(out[:, t : t + PARTS[h]], total[:])
+        sums = [keep.tile([P, T // 2], F32, name=f"sums{h}") for h in range(2)]
+
+        def add(h, lo, hi, pair, at):
+            nc.vector.tensor_tensor(sums[h][:, lo:hi], pair[0][:, at : at + hi - lo], pair[1][:, at : at + hi - lo], ADD)
 
         a1 = fetch(0, 0)
         a2 = fetch(1, 0)
         b1 = fetch(0, 1)
-        finish(0, a1, a2)
+        add(0, 0, 512, (a1, a2), 0)
+        nc.sync.dma_start(out[:, : T // 2], sums[0][:])
         b2 = fetch(1, 1)
-        finish(1, b1, b2)
+        add(1, 0, 256, (a1, a2), 512)
+        add(1, 256, 512, (b1, b2), 0)
+        nc.sync.dma_start(out[:, T // 2 :], sums[1][:])

from contextlib import ExitStack

import concourse.mybir as mybir

K, T, E, C, N = 1536, 1024, 16, 128, 128
FLOPS = 2 * K * N * E * C

F32 = mybir.dt.float32
BF16 = mybir.dt.bfloat16
I32 = mybir.dt.int32
U32 = mybir.dt.uint32
U16 = mybir.dt.uint16
U8 = mybir.dt.uint8
FP8X4 = mybir.dt.float8_e4m3fn_x4
MULT = mybir.AluOpType.mult
ADD = mybir.AluOpType.add

P = 128
PASSES = K // 512
LOADS = ((512, 256, 256), (256, 256, 512), (512, 512))
CASTS = ((("V", 0, 320), ("S", 320, 512), ("V", 512, 672), ("S", 672, 768), ("V", 768, 928), ("S", 928, 1024)), (("S", 0, 256), ("S", 256, 512), ("S", 512, 768), ("S", 768, 896), ("V", 896, 1024)), (("S", 0, 512), ("S", 512, 768), ("S", 768, 1024)))
QUANT = ((512, 256, 256), (512, 256, 128, 128), (512, 256, 256))
WORDS = ((12, 4), (12, 4), (6, 6, 3, 1))
BYTES_CUT = (6, 6, 4)
SEQ = ("q0", "w00", "w01", "q1", "w10", "w11", "q2", "b0", "w20", "b1", "w21", "b2", "w22", "w23")
VECTOR_COPIES = (15,)
WLOADS = (6, 6, 4)
PARTS = (768, 256)
SHARED = (1, 3)
WINDOWS = (2048, 2048, 1024)
SCALE_WINDOW = 2048


def tile_routed_moe_kernel(tc, xT, w_words, w_scales, gate, offs, pos1, pos2, out):
    nc = tc.nc
    with ExitStack() as ctx:
        keep = ctx.enter_context(tc.tile_pool(name="keep", bufs=1))
        turn = ctx.enter_context(tc.tile_pool(name="turn", bufs=1))
        psum = ctx.enter_context(tc.psum_pool(name="psum", bufs=1))

        offs_sb = keep.tile([P, E * C // 16], U16, name="offs_sb")
        pos_sb = [keep.tile([P, T // 16], U16, name=f"pos{i}_sb") for i in (1, 2)]
        x_pass = xT.rearrange("(g p t) n -> g p t n", p=P, t=4)
        x_code = [(turn if a == 0 else keep).tile([P, WINDOWS[a]], I32, name=f"x_code{a}", tag="turn" if a == 0 else f"x_code{a}", align_bytes=64) for a in range(PASSES)]
        x_scale = keep.tile([P, SCALE_WINDOW], U8, name="x_scale", align_bytes=64)
        w_scale = keep.tile([P, E, PASSES, N], U8, name="w_scale", align_bytes=64)
        nc.gpsimd.memset(x_scale[:], 0)
        for a in range(PASSES):
            if WINDOWS[a] > T:
                nc.vector.memset(x_code[a][:, T:], 0)
        nc.gpsimd.memset(w_scale[:].rearrange("p e a n -> p (e a n)").bitcast(I32), 0)

        def load_scales():
            for q in range(4):
                nc.sync.dma_start(
                    w_scale[32 * q : 32 * q + 4].rearrange("p e a n -> p (e a) n").bitcast(I32),
                    w_scales[:, :, 4 * q : 4 * q + 4, :].rearrange("e a q n -> q (e a) n").bitcast(I32),
                )

        raw = []
        for a in range(PASSES):
            parts = []
            col = 0
            for i, width in enumerate(LOADS[a]):
                r = keep.tile([P, 4, width], F32, name=f"raw{a}_{i}")
                nc.sync.dma_start(r[:], x_pass[a, :, :, col : col + width])
                if a == 0 and i == len(LOADS[0]) - 1:
                    nc.sync.dma_start(offs_sb[:], offs)
                parts.append((col, width, r))
                col += width
            raw.append(parts)

        w_at = []
        e0 = 0
        for c, ne in enumerate(WLOADS):
            if c == 0:
                load_scales()
            w = keep.tile([P, ne * PASSES, N], U32, name=f"w_code{c}", align_bytes=64)
            nc.sync.dma_start(w[:].bitcast(I32), w_words[e0 : e0 + ne].rearrange("e a p n r -> p (e a) (n r)").bitcast(I32))
            w_at += [(w, j) for j in range(ne)]
            e0 += ne
            if c == 0:
                nc.sync.dma_start(pos_sb[0][:], pos1)
                nc.sync.dma_start(pos_sb[1][:], pos2)
        gate_sb = [keep.tile([P, T], F32, name=f"gate{i}_sb") for i in (1, 2)]
        for i in range(2):
            nc.sync.dma_start(gate_sb[i][:], gate[i])

        code_at = [[] for a in range(PASSES)]
        scale_at = []

        def gather(window, cuts, c, dtype, name, where):
            e0, ne = sum(cuts[:c]), cuts[c]
            g = keep.tile([P, ne * C], dtype, name=name, align_bytes=64)
            nc.vector.tensor_copy(g[:], window.indirect(offs_sb[:, e0 * C // 16 : (e0 + ne) * C // 16]))
            where.extend((g, j * C) for j in range(ne))

        def quantise(a):
            q0 = 0
            for b, width in enumerate(QUANT[a]):
                shared = (a, b) == SHARED
                xb = (turn if shared else keep).tile([P, width, 4], BF16, name=f"xb{a}_{b}", tag="turn" if shared else f"xb{a}_{b}", align_bytes=64)
                for engine, lo, hi in CASTS[a]:
                    if not (q0 <= lo < q0 + width):
                        continue
                    for col, wd, r in raw[a]:
                        if col <= lo < col + wd:
                            copy = nc.vector.tensor_copy if engine == "V" else nc.scalar.copy
                            copy(
                                xb[:, lo - q0 : hi - q0, :].rearrange("p (c i) t -> p c t i", i=4),
                                r[:, :, lo - col : hi - col].rearrange("p t (c i) -> p c t i", i=4),
                            )
                cols = slice(q0, q0 + width)
                nc.vector.quantize_mx(
                    out=x_code[a][:, cols].bitcast(FP8X4),
                    scales=x_scale[4 * a : P, cols],
                    in_=xb[:].rearrange("p n t -> p (n t)"),
                )
                q0 += width

        y = keep.tile([P, E * C], F32, name="y")
        last = PASSES - 1
        accs = []

        def multiply(e, passes):
            sc, s0 = scale_at[e]
            w, wj = w_at[e]
            for a in passes:
                co, c0 = code_at[a][e]
                nc.tensor.matmul_mx(
                    out=accs[e][:],
                    lhsT=w[:, wj * PASSES + a, :].bitcast(FP8X4),
                    lhsT_scale=w_scale[:, e, a, :],
                    rhs=co[:, c0 : c0 + C].bitcast(FP8X4),
                    rhs_scale=sc[4 * a : P, s0 : s0 + C],
                    start=(a == 0),
                    stop=(a == last),
                )

        for what in SEQ:
            if what[0] == "q":
                quantise(int(what[1]))
            elif what[0] == "b":
                e0 = len(scale_at)
                gather(x_scale[:], BYTES_CUT, int(what[1]), U8, f"slot_scale{what[1]}", scale_at)
                for e in range(e0, len(scale_at)):
                    acc = psum.tile([P, C], F32, name=f"acc{e}", tag=f"bank{e % 8}")
                    accs.append(acc)
                    multiply(e, range(last))
            else:
                a = int(what[1])
                e0 = len(code_at[a])
                gather(x_code[a][:].bitcast(U32), WORDS[a], int(what[2]), U32, f"slot_code{a}_{what[2]}", code_at[a])
                if a == last:
                    for e in range(e0, len(code_at[a])):
                        multiply(e, [last])
                        copy = nc.vector.tensor_copy if e in VECTOR_COPIES else nc.scalar.copy
                        copy(y[:, e * C : (e + 1) * C], accs[e][:])

        def fetch(i, h):
            g = keep.tile([P, PARTS[h]], F32, name=f"part{i}_{h}")
            t = sum(PARTS[:h])
            nc.vector.tensor_tensor(
                g[:], y[:].indirect(pos_sb[i][:, t // 16 : (t + PARTS[h]) // 16]), gate_sb[i][:, t : t + PARTS[h]], MULT
            )
            return g

        sums = [keep.tile([P, T // 2], F32, name=f"sums{h}") for h in range(2)]

        def add(h, lo, hi, pair, at):
            nc.vector.tensor_tensor(sums[h][:, lo:hi], pair[0][:, at : at + hi - lo], pair[1][:, at : at + hi - lo], ADD)

        a1 = fetch(0, 0)
        a2 = fetch(1, 0)
        b1 = fetch(0, 1)
        add(0, 0, 512, (a1, a2), 0)
        nc.sync.dma_start(out[:, : T // 2], sums[0][:])
        b2 = fetch(1, 1)
        add(1, 0, 256, (a1, a2), 512)
        add(1, 256, 512, (b1, b2), 0)
        nc.sync.dma_start(out[:, T // 2 :], sums[1][:])
